import numpy as np, ml_dtypes
CORES = [10,34,74,98]
N = 4
import mx_ref
BF = ml_dtypes.bfloat16
def entries(a):
    return np.ascontiguousarray(a.T).reshape(-1)
def table(e):
    return np.ascontiguousarray(np.reshape(e, (-1, 16)).T).astype(np.int32)
def cut(t, i, w=512):
    return t[:, w * i:w * i + w]
def f(rng, *shape):
    return mx_ref.flush((rng.standard_normal(shape, dtype=np.float32) * np.exp2(rng.integers(-2, 3, shape[:-1] + (1,)))).astype(BF))
def wide(rng, *shape, cols=0):
    v = rng.standard_normal(shape, dtype=np.float32) * np.exp2(rng.integers(-12, 13, shape)).astype(np.float32)
    if cols: v *= np.repeat(np.exp2(rng.integers(-cols, cols + 1, shape[:-2] + (1, shape[-1] // 4))) * (rng.random(shape[:-2] + (1, shape[-1] // 4)) > 0.0625), 4, axis=-1).astype(np.float32)
    return mx_ref.flush(v.astype(BF))
E, NB = 4, 8
T, L, G = 128 * NB, 4 * NB, N * E
def listed(es):
    return {"ids": np.stack([table(e) for e in es])}
def setup_inputs(rng):
    return {"x": f(rng, N, 128, 4 * T), "wt": f(rng, N, 128, 512 * E), **listed([rng.integers(0, G, L) for r in range(N)])}
def setup_inputs_one(rng):
    return {**setup_inputs(rng), **listed([np.full(L, rng.integers(0, G))] * N)}
def setup_inputs_own(rng):
    return {**setup_inputs(rng), **listed([r * E + rng.integers(0, E, L) for r in range(N)])}
def setup_inputs_ends(rng):
    es = []
    for r in range(N):
        e = rng.choice([0, G - 1], L); e[rng.permutation(L)[:2]] = [0, G - 1]
        es.append(e)
    return {**setup_inputs(rng), **listed(es)}
def setup_inputs_each(rng):
    return {**setup_inputs(rng), **listed([np.concatenate([rng.permutation(G) for i in range(L // G + 1)])[:L] for r in range(N)])}
def setup_inputs_spread(rng):
    d = setup_inputs(rng); d["x"] = wide(rng, N, 128, 4 * T, cols=8); d["wt"] = wide(rng, N, 128, 512 * E, cols=8); return d
def check_inputs(d):
    b = []
    for r in range(N):
        e = entries(d["ids"][r])
        if e.min() < 0 or e.max() >= G: b.append("ids")
    return b
def reference(x, wt, ids):
    U = [mx_ref.quantize(np.ascontiguousarray(cut(wt[q], m))) for q in range(N) for m in range(E)]
    y = np.zeros((N, 128, 4 * T), np.float32)
    for r in range(N):
        e = entries(ids[r])
        for b in range(NB):
            X = mx_ref.quantize(np.ascontiguousarray(cut(x[r], b)))
            for k in range(4):
                c = 128 * (k * NB + b)
                y[r][:, c:c + 128] = mx_ref.matmul(U[e[4 * b + k]], X)
    return {"y": y}

@@ -1,0 +1,232 @@
+from concourse.bass import DstId, RemoteDMATransfer
+from concourse.mybir import dt, AluOpType, ActivationFunctionType
+
+NR, TILES, NBLK, CH = 4, 4, 8, 4
+CW = 32
+PART = TILES * CW
+COPY = ActivationFunctionType.Copy
+
+SCRATCH = {
+    "wn": ("sbuf", [128, 2048], "bfloat16"),
+    "xb": ("sbuf", [128, 4096], "bfloat16"),
+    "xq": ("sbuf", [128, 1024], "float8_e4m3fn_x4"),
+    "xs": ("sbuf", [128, 1024], "uint8"),
+    "idr": ("sbuf", [128, 32], "int32"),
+    "idb": ("sbuf", [128, 32], "int32"),
+    "idf": ("sbuf", [128, 32], "float32"),
+    "ka": ("sbuf", [128, 32], "int32"),
+    "kb": ("sbuf", [128, 32], "int32"),
+    "km": ("sbuf", [128, 32], "float32"),
+    "pa": ("sbuf", [128, 2], "int32"),
+    "pb": ("sbuf", [128, 2], "int32"),
+    "pu": ("sbuf", [128, 2], "float32"),
+    "ea": ("sbuf", [128, 32], "float32"),
+    "eb": ("sbuf", [128, 28], "float32"),
+    "sel": ("sbuf", [128, 8], "float32"),
+    "off": ("sbuf", [128, 64], "uint16"),
+    "ps": ("psum", [128, 4096], "float32"),
+}
+for _c in range(CH):
+    SCRATCH["w%d" % _c] = ("sbuf", [128, 512], "bfloat16")
+    SCRATCH["cw%d" % _c] = ("sbuf", [128, NR * PART], "float8_e4m3fn_x4")
+    SCRATCH["cs%d" % _c] = ("sbuf", [128, NR * PART], "uint8")
+    SCRATCH["pk%d" % _c] = ("sbuf", [128, 1024], "float8_e4m3fn_x4")
+    SCRATCH["pp%d" % _c] = ("sbuf", [128, 1024], "uint8")
+    SCRATCH["yo%d" % _c] = ("sbuf", [128, 1024], "float32")
+
+SEMAPHORES = ["idl", "wl0", "wl1", "xl0", "xl1", "ga", "va", "sa", "ta", "loc", "hc", "hs", "out"] \
+    + ["ac%d" % c for c in range(CH)] + ["as%d" % c for c in range(CH)]
+
+
+def bits(es):
+    return sum(1 << e for e in es)
+
+
+def part(T, kind, c, r):
+    v = T["%s%d" % (kind, c)][:, PART * r:PART * r + PART]
+    return v.bitcast(dt.uint8) if kind == "cw" else v
+
+
+def send(T, topo, kind, c, r, dsts, es, sem):
+    ids = []
+    for d in dsts:
+        rid, pid, _s = topo.addr(d)
+        ids.append(DstId(rid=rid, pnc=pid))
+    return RemoteDMATransfer(dst_ids=ids, dma_engine_mask=bits(es), remote_sem=T.sem[sem],
+                             srcs=[part(T, kind, c, r)], dsts=[part(T, kind, c, r) for d in dsts])
+
+
+def others(T, r):
+    return [T.cores[(r + i) % NR] for i in range(1, NR)]
+
+
+def relays(T, topo, r):
+    me = T.cores[r]
+    ok = [c for c in topo.cores_of(me) if c != me and all(topo.may_write(c, d) for d in others(T, r))]
+    near = [c for c in ok if topo.die(c) == topo.die(me)]
+    far = [c for c in ok if topo.die(c) != topo.die(me)]
+    return near[:1] + far[:2]
+
+
+def relay_engines(T, topo, r):
+    me = T.cores[r]
+    far = topo.engines(me, others(T, r)[0])
+    spare = [e for e in topo.engines(me, relays(T, topo, r)[0]) if e not in far]
+    h = len(spare) // 2
+    return [spare[:h], spare[h:], far[:h]]
+
+
+def relay_program(g, core, T, topo, r, c):
+    dsts = others(T, r)
+    es = topo.engines(core, dsts[0])
+    n = len(relay_engines(T, topo, r)[c - 1])
+    g.wait_ge(T.sem.hc, n)
+    g.remote_dma_fused([send(T, topo, "cw", c, r, dsts, es, "ac%d" % c)], local_sem=T.sem.loc)
+    g.wait_ge(T.sem.hs, n)
+    g.remote_dma_fused([send(T, topo, "cs", c, r, dsts, es, "as%d" % c)], local_sem=T.sem.loc)
+    g.wait_ge(T.sem.loc, 2 * len(es))
+
+
+def rank_program(g, core, T, topo):
+    r = T.rank_of(core)
+    if r is None:
+        for q in range(NR):
+            hs = relays(T, topo, q)
+            if core in hs:
+                relay_program(g, core, T, topo, q, 1 + hs.index(core))
+        return
+    S = T.sem
+    V, A, P, Y = g.vector, g.scalar, g.tensor, g.sync
+    nv, na = [0], [0]
+
+    def v(ins):
+        ins.then_inc(S.va, 1)
+        nv[0] += 1
+        return nv[0]
+
+    def a(ins):
+        ins.then_inc(S.sa, 1)
+        na[0] += 1
+        return na[0]
+
+    Y.dma_start(T.idr[0:1, 0:32], T.ids[:, :]).then_inc(S.idl, 16)
+    for m in range(TILES):
+        (Y if m < 2 else A).dma_start(T.w0[:, 128 * m:128 * m + 128], T.wt[:, 512 * m:512 * m + 128]).then_inc(S.wl0, 16)
+    for m in range(TILES):
+        (Y if m < 2 else A).dma_start(T.wn[:, 512 * m + 128:512 * m + 512], T.wt[:, 512 * m + 128:512 * m + 512]).then_inc(S.wl1, 16)
+    Y.dma_start(T.xb[:, 0:2048], T.x[:, 0:2048]).then_inc(S.xl0, 16)
+    A.dma_start(T.xb[:, 2048:4096], T.x[:, 2048:4096]).then_inc(S.xl1, 16)
+
+    dsts = others(T, r)
+    hs = relays(T, topo, r)
+    far = topo.engines(core, dsts[0])
+    near = relay_engines(T, topo, r)
+    g.iota(T.ka[:, :], [[0, 4], [1, 4], [0, 2]], 0, 3).then_inc(S.ga, 1)
+    g.iota(T.pa[:, :], [[0, 2]], 0, 1).then_inc(S.ga, 1)
+    g.wait_ge(S.idl, 16)
+    g.partition_broadcast(T.idb[:, :], T.idr[0:1, :], 128).then_inc(S.ga, 1)
+
+    V.wait_ge(S.ga, 2)
+    v(V.tensor_scalar(T.kb[:, :], T.ka[:, :], 3, None, AluOpType.bitwise_and))
+    n = v(V.tensor_scalar(T.pb[:, :], T.pa[:, :], 2, 3, AluOpType.logical_shift_right, AluOpType.bitwise_and))
+    V.wait_ge(S.va, n)
+    v(V.tensor_scalar(T.km[:, :], T.kb[:, :], 0, CW, AluOpType.is_equal, AluOpType.mult))
+    n = v(V.tensor_copy(T.pu[:, :], T.pb[:, :]))
+    V.wait_ge(S.va, n)
+    quant = [0] * CH
+    lo, hi = PART * r, PART * r + PART
+    V.wait_ge(S.wl0, 64)
+    quant[0] = v(V.quantize_mx(T.cw0[:, lo:hi], T.cs0[:, lo:hi], T.w0[:, :]))
+    V.wait_ge(S.ga, 3)
+    n = v(V.tensor_copy(T.idf[:, :], T.idb[:, :]))
+    V.wait_ge(S.va, n)
+    n = v(V.tensor_tensor(T.ea[:, :], T.idf[:, :], T.km[:, :], AluOpType.mult))
+    V.wait_ge(S.va, n)
+    n = v(V.tensor_tensor(T.eb[:, :], T.ea[:, 0:28], T.ea[:, 4:32], AluOpType.add))
+    V.wait_ge(S.va, n)
+    for h in range(2):
+        n = v(V.tensor_tensor(T.sel[:, 4 * h:4 * h + 4], T.eb[:, h:h + 25:8], T.eb[:, h + 2:h + 27:8], AluOpType.add))
+    V.wait_ge(S.va, n)
+    for ii in range(8):
+        listed = v(V.tensor_scalar(T.off[:, ii:64:8], T.sel[:, :], T.pu[:, 0:1], 4 * ii, AluOpType.add, AluOpType.add))
+    A.wait_ge(S.wl1, 64)
+    for m in range(TILES):
+        moved = a(A.activation(T.w3[:, 128 * m:128 * m + 128], T.wn[:, 512 * m + 384:512 * m + 512], COPY))
+    V.wait_ge(S.wl1, 64)
+    for c in (1, 2, 3):
+        if c < 3:
+            for m in range(TILES):
+                n = v(V.tensor_copy(T["w%d" % c][:, 128 * m:128 * m + 128], T.wn[:, 512 * m + 128 * c:512 * m + 128 * c + 128]))
+            V.wait_ge(S.va, n)
+        else:
+            V.wait_ge(S.sa, moved)
+        quant[c] = v(V.quantize_mx(T["cw%d" % c][:, lo:hi], T["cs%d" % c][:, lo:hi], T["w%d" % c][:, :]))
+    for h in range(2):
+        V.wait_ge(S["xl%d" % h], 16)
+        xdone = v(V.quantize_mx(T.xq[:, 512 * h:512 * h + 512], T.xs[:, 512 * h:512 * h + 512], T.xb[:, 2048 * h:2048 * h + 2048]))
+
+    g.wait_ge(S.va, quant[0])
+    g.remote_dma_fused([send(T, topo, "cw", 0, r, dsts, far, "ac0")], local_sem=S.loc)
+    g.remote_dma_fused([send(T, topo, "cs", 0, r, dsts, far, "as0")], local_sem=S.loc)
+    g.wait_ge(S.va, quant[3])
+    g.remote_dma_fused([send(T, topo, "cw", c, r, [hs[c - 1]], near[c - 1], "hc") for c in (1, 2, 3)], local_sem=S.loc)
+    g.remote_dma_fused([send(T, topo, "cs", c, r, [hs[c - 1]], near[c - 1], "hs") for c in (1, 2, 3)], local_sem=S.loc)
+    g.wait_ge(S.loc, 2 * len(far) + 2 * sum(len(e) for e in near))
+
+    nin = (NR - 1) * len(far)
+    pickv, picka, copyv, copya = {}, {}, {}, {}
+
+    def copies(c, u):
+        b = 2 * u
+        V.wait_ge(S.ta, 8 * c + b + 1)
+        copyv[c, u] = v(V.tensor_copy(T["yo%d" % c][:, 128 * b:128 * b + 128], T.ps[:, 512 * b:512 * b + 128]))
+        b = 2 * u + 1
+        A.wait_ge(S.ta, 8 * c + b + 1)
+        copya[c, u] = a(A.activation(T["yo%d" % c][:, 128 * b:128 * b + 128], T.ps[:, 512 * b:512 * b + 128], COPY))
+
+    V.wait_ge(S.va, xdone)
+    A.wait_ge(S.va, xdone)
+    due = []
+    for c in range(CH):
+        V.wait_ge(S["ac%d" % c], nin)
+        A.wait_ge(S["as%d" % c], nin)
+        for u in range(4):
+            o, w = T.off[:, 16 * u:16 * u + 16], slice(256 * u, 256 * u + 256)
+            pickv[c, u] = v(V.tensor_copy(T["pk%d" % c][:, w].bitcast(dt.uint32), T["cw%d" % c][:, 0:512].bitcast(dt.uint32).indirect(o)))
+            picka[c, u] = a(A.activation(T["pp%d" % c][:, w], T["cs%d" % c][:, 0:512].indirect(o), COPY))
+            for d in due:
+                copies(*d)
+            due = [(c, u)]
+    for d in due:
+        copies(*d)
+
+    P.wait_ge(S.va, xdone)
+    for c in range(CH):
+        for u in range(4):
+            P.wait_ge(S.va, pickv[c, u])
+            P.wait_ge(S.sa, picka[c, u])
+            if c:
+                P.wait_ge(S.va, copyv[c - 1, u])
+                P.wait_ge(S.sa, copya[c - 1, u])
+            for b in (2 * u, 2 * u + 1):
+                w = slice(128 * b, 128 * b + 128)
+                P.matmul_mx(T.ps[:, 512 * b:512 * b + 128], T["pk%d" % c][:, w], T["pp%d" % c][:, w],
+                            T.xq[:, w], T.xs[:, w], True, True).then_inc(S.ta, 1)
+
+    for c in range(CH - 1):
+        Y.wait_ge(S.va, copyv[c, 3])
+        Y.wait_ge(S.sa, copya[c, 3])
+        Y.dma_start(T.y[32 * c:32 * c + 32, :], T["yo%d" % c][:, :]).then_inc(S.out, 16)
+    c = CH - 1
+    for h in range(2):
+        Y.wait_ge(S.va, copyv[c, 2 * h + 1])
+        Y.wait_ge(S.sa, copya[c, 2 * h + 1])
+        if h:
+            A.wait_ge(S.va, copyv[c, 3])
+            A.wait_ge(S.sa, copya[c, 3])
+        for k in range(4):
+            q = A if h and k % 2 else Y
+            q.dma_start(T.y[32 * c:32 * c + 32, 1024 * k + 512 * h:1024 * k + 512 * h + 512],
+                        T["yo%d" % c][k:128:4, 512 * h:512 * h + 512]).then_inc(S.out, 16)
+    Y.wait_ge(S.ta, 8 * CH)
+    Y.wait_ge(S.out, 16 * (CH - 1 + 8))

@@ -4,7 +4,10 @@ from concourse.mybir import dt, AluOpType, ActivationFunctionType
 NR, TILES, NBLK, CH = 4, 4, 8, 4
 CW = 32
 PART = TILES * CW
-COPY = ActivationFunctionType.Copy
+COPY, IDENT = ActivationFunctionType.Copy, ActivationFunctionType.Identity
+UNIT = 2
+PIECES = {0: (4, 4), 1: (4, 4), 2: (4, 4), 3: (2, 2, 2, 2)}
+XLATE = 3
 
 SCRATCH = {
     "wn": ("sbuf", [128, 2048], "bfloat16"),
@@ -17,24 +20,27 @@ SCRATCH = {
     "ka": ("sbuf", [128, 32], "int32"),
     "kb": ("sbuf", [128, 32], "int32"),
     "km": ("sbuf", [128, 32], "float32"),
-    "pa": ("sbuf", [128, 2], "int32"),
-    "pb": ("sbuf", [128, 2], "int32"),
-    "pu": ("sbuf", [128, 2], "float32"),
+    "pa": ("sbuf", [128, 8], "int32"),
+    "pb": ("sbuf", [128, 8], "int32"),
+    "ia": ("sbuf", [128, 8], "int32"),
+    "pu": ("sbuf", [128, 8], "float32"),
     "ea": ("sbuf", [128, 32], "float32"),
     "eb": ("sbuf", [128, 28], "float32"),
     "sel": ("sbuf", [128, 8], "float32"),
+    "offf": ("sbuf", [128, 64], "float32"),
     "off": ("sbuf", [128, 64], "uint16"),
     "ps": ("psum", [128, 4096], "float32"),
 }
 for _c in range(CH):
-    SCRATCH["w%d" % _c] = ("sbuf", [128, 512], "bfloat16")
     SCRATCH["cw%d" % _c] = ("sbuf", [128, NR * PART], "float8_e4m3fn_x4")
     SCRATCH["cs%d" % _c] = ("sbuf", [128, NR * PART], "uint8")
+    SCRATCH["w%d" % _c] = ("sbuf", [128, 512], "bfloat16")
     SCRATCH["pk%d" % _c] = ("sbuf", [128, 1024], "float8_e4m3fn_x4")
     SCRATCH["pp%d" % _c] = ("sbuf", [128, 1024], "uint8")
     SCRATCH["yo%d" % _c] = ("sbuf", [128, 1024], "float32")
 
-SEMAPHORES = ["idl", "wl0", "wl1", "xl0", "xl1", "ga", "va", "sa", "ta", "loc", "hc", "hs", "out"] \
+SEMAPHORES = ["idl", "wl0", "wl1", "xl0", "xl1", "ga", "va", "sa", "ta", "loc", "out"] \
+    + ["hc%d" % c for c in range(CH)] + ["hs%d" % c for c in range(CH)] \
     + ["ac%d" % c for c in range(CH)] + ["as%d" % c for c in range(CH)]
 
 
@@ -49,11 +55,11 @@ def part(T, kind, c, r):
 
 def send(T, topo, kind, c, r, dsts, es, sem):
     ids = []
-    for d in dsts:
-        rid, pid, _s = topo.addr(d)
+    for q in dsts:
+        rid, pid, _s = topo.addr(q)
         ids.append(DstId(rid=rid, pnc=pid))
-    return RemoteDMATransfer(dst_ids=ids, dma_engine_mask=bits(es), remote_sem=T.sem[sem],
-                             srcs=[part(T, kind, c, r)], dsts=[part(T, kind, c, r) for d in dsts])
+    return RemoteDMATransfer(dst_ids=ids, dma_engine_mask=bits(es), remote_sem=T.sem["%s%d" % (sem, c)],
+                             srcs=[part(T, kind, c, r)], dsts=[part(T, kind, c, r) for q in dsts])
 
 
 def others(T, r):
@@ -65,26 +71,29 @@ def relays(T, topo, r):
     ok = [c for c in topo.cores_of(me) if c != me and all(topo.may_write(c, d) for d in others(T, r))]
     near = [c for c in ok if topo.die(c) == topo.die(me)]
     far = [c for c in ok if topo.die(c) != topo.die(me)]
-    return near[:1] + far[:2]
+    return far[:2] + near[:1]
 
 
-def relay_engines(T, topo, r):
+def on_chip(T, topo, r):
     me = T.cores[r]
-    far = topo.engines(me, others(T, r)[0])
-    spare = [e for e in topo.engines(me, relays(T, topo, r)[0]) if e not in far]
-    h = len(spare) // 2
-    return [spare[:h], spare[h:], far[:h]]
+    off = topo.engines(me, others(T, r)[0])
+    sp = [e for e in topo.engines(me, relays(T, topo, r)[0]) if e not in off]
+    h, q = len(sp) // 2, 3 * len(sp) // 4
+    return [[("cw", 2, 0, sp[:h]), ("cw", 3, 1, sp[h:])],
+            [("cs", 1, 2, sp[:h]), ("cs", 2, 2, sp[h:q]), ("cs", 3, 1, sp[q:])]]
 
 
-def relay_program(g, core, T, topo, r, c):
+def relay_program(g, core, T, topo, r, i):
     dsts = others(T, r)
     es = topo.engines(core, dsts[0])
-    n = len(relay_engines(T, topo, r)[c - 1])
-    g.wait_ge(T.sem.hc, n)
-    g.remote_dma_fused([send(T, topo, "cw", c, r, dsts, es, "ac%d" % c)], local_sem=T.sem.loc)
-    g.wait_ge(T.sem.hs, n)
-    g.remote_dma_fused([send(T, topo, "cs", c, r, dsts, es, "as%d" % c)], local_sem=T.sem.loc)
-    g.wait_ge(T.sem.loc, 2 * len(es))
+    n = 0
+    for call in on_chip(T, topo, r):
+        for kind, c, j, got in call:
+            if j == i:
+                g.wait_ge(T.sem["h%s%d" % (kind[1].replace("w", "c"), c)], len(got))
+                g.remote_dma_fused([send(T, topo, kind, c, r, dsts, es, "ac" if kind == "cw" else "as")], local_sem=T.sem.loc)
+                n += len(es)
+    g.wait_ge(T.sem.loc, n)
 
 
 def rank_program(g, core, T, topo):
@@ -93,7 +102,7 @@ def rank_program(g, core, T, topo):
         for q in range(NR):
             hs = relays(T, topo, q)
             if core in hs:
-                relay_program(g, core, T, topo, q, 1 + hs.index(core))
+                relay_program(g, core, T, topo, q, hs.index(core))
         return
     S = T.sem
     V, A, P, Y = g.vector, g.scalar, g.tensor, g.sync
@@ -109,124 +118,144 @@ def rank_program(g, core, T, topo):
         na[0] += 1
         return na[0]
 
-    Y.dma_start(T.idr[0:1, 0:32], T.ids[:, :]).then_inc(S.idl, 16)
     for m in range(TILES):
         (Y if m < 2 else A).dma_start(T.w0[:, 128 * m:128 * m + 128], T.wt[:, 512 * m:512 * m + 128]).then_inc(S.wl0, 16)
     for m in range(TILES):
         (Y if m < 2 else A).dma_start(T.wn[:, 512 * m + 128:512 * m + 512], T.wt[:, 512 * m + 128:512 * m + 512]).then_inc(S.wl1, 16)
-    Y.dma_start(T.xb[:, 0:2048], T.x[:, 0:2048]).then_inc(S.xl0, 16)
+    Y.dma_start(T.idr[0:1, 0:32], T.ids[:, :]).then_inc(S.idl, 16)
     A.dma_start(T.xb[:, 2048:4096], T.x[:, 2048:4096]).then_inc(S.xl1, 16)
+    Y.dma_start(T.xb[:, 0:2048], T.x[:, 0:2048]).then_inc(S.xl0, 16)
 
     dsts = others(T, r)
     hs = relays(T, topo, r)
     far = topo.engines(core, dsts[0])
-    near = relay_engines(T, topo, r)
     g.iota(T.ka[:, :], [[0, 4], [1, 4], [0, 2]], 0, 3).then_inc(S.ga, 1)
-    g.iota(T.pa[:, :], [[0, 2]], 0, 1).then_inc(S.ga, 1)
-    g.wait_ge(S.idl, 16)
-    g.partition_broadcast(T.idb[:, :], T.idr[0:1, :], 128).then_inc(S.ga, 1)
+    g.iota(T.pa[:, :], [[0, 8]], 0, 1).then_inc(S.ga, 1)
+    g.iota(T.ia[:, :], [[4, 8]], 0, 0).then_inc(S.ga, 1)
 
-    V.wait_ge(S.ga, 2)
+    V.wait_ge(S.ga, 3)
     v(V.tensor_scalar(T.kb[:, :], T.ka[:, :], 3, None, AluOpType.bitwise_and))
     n = v(V.tensor_scalar(T.pb[:, :], T.pa[:, :], 2, 3, AluOpType.logical_shift_right, AluOpType.bitwise_and))
     V.wait_ge(S.va, n)
     v(V.tensor_scalar(T.km[:, :], T.kb[:, :], 0, CW, AluOpType.is_equal, AluOpType.mult))
-    n = v(V.tensor_copy(T.pu[:, :], T.pb[:, :]))
-    V.wait_ge(S.va, n)
-    quant = [0] * CH
-    lo, hi = PART * r, PART * r + PART
-    V.wait_ge(S.wl0, 64)
-    quant[0] = v(V.quantize_mx(T.cw0[:, lo:hi], T.cs0[:, lo:hi], T.w0[:, :]))
-    V.wait_ge(S.ga, 3)
+    v(V.tensor_tensor(T.pu[:, :], T.pb[:, :], T.ia[:, :], AluOpType.add))
+
+    quant = {}
+    cols = slice(PART * r, PART * r + PART)
+
+    def quantise(c):
+        quant[c] = v(V.quantize_mx(T["cw%d" % c][:, cols], T["cs%d" % c][:, cols], T["w%d" % c][:, :]))
+
+    V.wait_ge(S.wl0, 16 * TILES)
+    quantise(0)
+    A.wait_ge(S.wl1, 16 * TILES)
+    for m in range(TILES):
+        moved = a(A.activation(T.w3[:, 128 * m:128 * m + 128], T.wn[:, 512 * m + 384:512 * m + 512], COPY))
+    V.wait_ge(S.wl1, 16 * TILES)
+    for c in (2, 3, 1):
+        if c != 3:
+            for m in range(TILES):
+                n = v(V.tensor_copy(T["w%d" % c][:, 128 * m:128 * m + 128], T.wn[:, 512 * m + 128 * c:512 * m + 128 * c + 128]))
+            V.wait_ge(S.va, n)
+        else:
+            V.wait_ge(S.sa, moved)
+        quantise(c)
+
+    g.wait_ge(S.va, quant[0])
+    g.remote_dma_fused([send(T, topo, "cw", 0, r, dsts, far, "ac")], local_sem=S.loc)
+    g.remote_dma_fused([send(T, topo, "cs", 0, r, dsts, far, "as")], local_sem=S.loc)
+    left = 3 * len(far)
+    for call, c in zip(on_chip(T, topo, r), (3, 1)):
+        g.wait_ge(S.va, quant[c])
+        g.remote_dma_fused([send(T, topo, kind, k, r, [hs[j]], es, "hc" if kind == "cw" else "hs") for kind, k, j, es in call], local_sem=S.loc)
+        left += sum(len(es) for _k, _c, _j, es in call)
+    g.remote_dma_fused([send(T, topo, "cw", 1, r, dsts, far, "ac")], local_sem=S.loc)
+    g.wait_ge(S.idl, 16)
+    g.partition_broadcast(T.idb[:, :], T.idr[0:1, :], 128).then_inc(S.ga, 1)
+    g.wait_ge(S.loc, left)
+
+    V.wait_ge(S.ga, 4)
     n = v(V.tensor_copy(T.idf[:, :], T.idb[:, :]))
     V.wait_ge(S.va, n)
     n = v(V.tensor_tensor(T.ea[:, :], T.idf[:, :], T.km[:, :], AluOpType.mult))
     V.wait_ge(S.va, n)
     n = v(V.tensor_tensor(T.eb[:, :], T.ea[:, 0:28], T.ea[:, 4:32], AluOpType.add))
     V.wait_ge(S.va, n)
-    for h in range(2):
-        n = v(V.tensor_tensor(T.sel[:, 4 * h:4 * h + 4], T.eb[:, h:h + 25:8], T.eb[:, h + 2:h + 27:8], AluOpType.add))
-    V.wait_ge(S.va, n)
+    for q in range(2):
+        n = v(V.tensor_tensor(T.sel[:, 4 * q:4 * q + 4], T.eb[:, q:q + 25:8], T.eb[:, q + 2:q + 27:8], AluOpType.add))
+    A.wait_ge(S.va, n)
     for ii in range(8):
-        listed = v(V.tensor_scalar(T.off[:, ii:64:8], T.sel[:, :], T.pu[:, 0:1], 4 * ii, AluOpType.add, AluOpType.add))
-    A.wait_ge(S.wl1, 64)
-    for m in range(TILES):
-        moved = a(A.activation(T.w3[:, 128 * m:128 * m + 128], T.wn[:, 512 * m + 384:512 * m + 512], COPY))
-    V.wait_ge(S.wl1, 64)
-    for c in (1, 2, 3):
-        if c < 3:
-            for m in range(TILES):
-                n = v(V.tensor_copy(T["w%d" % c][:, 128 * m:128 * m + 128], T.wn[:, 512 * m + 128 * c:512 * m + 128 * c + 128]))
-            V.wait_ge(S.va, n)
-        else:
-            V.wait_ge(S.sa, moved)
-        quant[c] = v(V.quantize_mx(T["cw%d" % c][:, lo:hi], T["cs%d" % c][:, lo:hi], T["w%d" % c][:, :]))
-    for h in range(2):
-        V.wait_ge(S["xl%d" % h], 16)
-        xdone = v(V.quantize_mx(T.xq[:, 512 * h:512 * h + 512], T.xs[:, 512 * h:512 * h + 512], T.xb[:, 2048 * h:2048 * h + 2048]))
+        m = a(A.activation(T.offf[:, ii:64:8], T.sel[:, :], IDENT, bias=T.pu[:, ii:ii + 1]))
+    xdone = {}
 
-    g.wait_ge(S.va, quant[0])
-    g.remote_dma_fused([send(T, topo, "cw", 0, r, dsts, far, "ac0")], local_sem=S.loc)
-    g.remote_dma_fused([send(T, topo, "cs", 0, r, dsts, far, "as0")], local_sem=S.loc)
-    g.wait_ge(S.va, quant[3])
-    g.remote_dma_fused([send(T, topo, "cw", c, r, [hs[c - 1]], near[c - 1], "hc") for c in (1, 2, 3)], local_sem=S.loc)
-    g.remote_dma_fused([send(T, topo, "cs", c, r, [hs[c - 1]], near[c - 1], "hs") for c in (1, 2, 3)], local_sem=S.loc)
-    g.wait_ge(S.loc, 2 * len(far) + 2 * sum(len(e) for e in near))
+    def quantise_x(q):
+        V.wait_ge(S["xl%d" % q], 16)
+        cs = slice(512 * q, 512 * q + 512)
+        xdone[q] = v(V.quantize_mx(T.xq[:, cs], T.xs[:, cs], T.xb[:, 2048 * q:2048 * q + 2048]))
+
+    quantise_x(0)
+    V.wait_ge(S.sa, m)
+    listed = v(V.tensor_copy(T.off[:, :], T.offf[:, :]))
 
     nin = (NR - 1) * len(far)
     pickv, picka, copyv, copya = {}, {}, {}, {}
 
-    def copies(c, u):
-        b = 2 * u
-        V.wait_ge(S.ta, 8 * c + b + 1)
-        copyv[c, u] = v(V.tensor_copy(T["yo%d" % c][:, 128 * b:128 * b + 128], T.ps[:, 512 * b:512 * b + 128]))
-        b = 2 * u + 1
-        A.wait_ge(S.ta, 8 * c + b + 1)
-        copya[c, u] = a(A.activation(T["yo%d" % c][:, 128 * b:128 * b + 128], T.ps[:, 512 * b:512 * b + 128], COPY))
+    def copies(c, b0):
+        for b in range(b0, b0 + UNIT):
+            o, i = T["yo%d" % c][:, 128 * b:128 * b + 128], T.ps[:, 512 * b:512 * b + 128]
+            if b % 2 == 0:
+                V.wait_ge(S.ta, NBLK * c + b + 1)
+                copyv[c, b] = v(V.tensor_copy(o, i))
+            else:
+                A.wait_ge(S.ta, NBLK * c + b + 1)
+                copya[c, b] = a(A.activation(o, i, COPY))
 
-    V.wait_ge(S.va, xdone)
-    A.wait_ge(S.va, xdone)
-    due = []
+    V.wait_ge(S.va, listed)
+    A.wait_ge(S.va, listed)
+    due, picks = [], 0
     for c in range(CH):
         V.wait_ge(S["ac%d" % c], nin)
         A.wait_ge(S["as%d" % c], nin)
-        for u in range(4):
-            o, w = T.off[:, 16 * u:16 * u + 16], slice(256 * u, 256 * u + 256)
-            pickv[c, u] = v(V.tensor_copy(T["pk%d" % c][:, w].bitcast(dt.uint32), T["cw%d" % c][:, 0:512].bitcast(dt.uint32).indirect(o)))
-            picka[c, u] = a(A.activation(T["pp%d" % c][:, w], T["cs%d" % c][:, 0:512].indirect(o), COPY))
+        for b0 in range(0, NBLK, UNIT):
+            o, to = T.off[:, 8 * b0:8 * b0 + 8 * UNIT], slice(128 * b0, 128 * b0 + 128 * UNIT)
+            pickv[c, b0] = v(V.tensor_copy(T["pk%d" % c][:, to].bitcast(dt.uint32), T["cw%d" % c][:, 0:NR * PART].bitcast(dt.uint32).indirect(o)))
+            picka[c, b0] = a(A.activation(T["pp%d" % c][:, to], T["cs%d" % c][:, 0:NR * PART].indirect(o), COPY))
+            picks += 1
+            if picks == XLATE:
+                quantise_x(1)
             for d in due:
                 copies(*d)
-            due = [(c, u)]
+            due = [(c, b0)]
     for d in due:
         copies(*d)
 
-    P.wait_ge(S.va, xdone)
     for c in range(CH):
-        for u in range(4):
-            P.wait_ge(S.va, pickv[c, u])
-            P.wait_ge(S.sa, picka[c, u])
-            if c:
-                P.wait_ge(S.va, copyv[c - 1, u])
-                P.wait_ge(S.sa, copya[c - 1, u])
-            for b in (2 * u, 2 * u + 1):
-                w = slice(128 * b, 128 * b + 128)
-                P.matmul_mx(T.ps[:, 512 * b:512 * b + 128], T["pk%d" % c][:, w], T["pp%d" % c][:, w],
-                            T.xq[:, w], T.xs[:, w], True, True).then_inc(S.ta, 1)
+        for b0 in range(0, NBLK, UNIT):
+            P.wait_ge(S.va, max(pickv[c, b0], xdone[2 * b0 // NBLK]))
+            P.wait_ge(S.sa, picka[c, b0])
+            for b in range(b0, b0 + UNIT):
+                if c:
+                    if b % 2 == 0:
+                        P.wait_ge(S.va, copyv[c - 1, b])
+                    else:
+                        P.wait_ge(S.sa, copya[c - 1, b])
+                cs = slice(128 * b, 128 * b + 128)
+                P.matmul_mx(T.ps[:, 512 * b:512 * b + 128], T["pk%d" % c][:, cs], T["pp%d" % c][:, cs],
+                            T.xq[:, cs], T.xs[:, cs], True, True).then_inc(S.ta, 1)
 
-    for c in range(CH - 1):
-        Y.wait_ge(S.va, copyv[c, 3])
-        Y.wait_ge(S.sa, copya[c, 3])
-        Y.dma_start(T.y[32 * c:32 * c + 32, :], T["yo%d" % c][:, :]).then_inc(S.out, 16)
-    c = CH - 1
-    for h in range(2):
-        Y.wait_ge(S.va, copyv[c, 2 * h + 1])
-        Y.wait_ge(S.sa, copya[c, 2 * h + 1])
-        if h:
-            A.wait_ge(S.va, copyv[c, 3])
-            A.wait_ge(S.sa, copya[c, 3])
-        for k in range(4):
-            q = A if h and k % 2 else Y
-            q.dma_start(T.y[32 * c:32 * c + 32, 1024 * k + 512 * h:1024 * k + 512 * h + 512],
-                        T["yo%d" % c][k:128:4, 512 * h:512 * h + 512]).then_inc(S.out, 16)
-    Y.wait_ge(S.ta, 8 * CH)
-    Y.wait_ge(S.out, 16 * (CH - 1 + 8))
+    nout = 0
+    for c in range(CH):
+        b0 = 0
+        for nb in PIECES[c]:
+            last = c == CH - 1 and b0 + nb == NBLK
+            for q in (Y, A) if last else (Y,):
+                q.wait_ge(S.va, copyv[c, b0 + nb - 2])
+                q.wait_ge(S.sa, copya[c, b0 + nb - 1])
+            for k in range(4):
+                (A if last and k % 2 else Y).dma_start(
+                    T.y[32 * c:32 * c + 32, 1024 * k + 128 * b0:1024 * k + 128 * (b0 + nb)],
+                    T["yo%d" % c][k:128:4, 128 * b0:128 * (b0 + nb)]).then_inc(S.out, 16)
+                nout += 1
+            b0 += nb
+    Y.wait_ge(S.ta, NBLK * CH)
+    Y.wait_ge(S.out, 16 * nout)

from concourse.bass import DstId, RemoteDMATransfer
from concourse.mybir import dt, AluOpType, ActivationFunctionType

NR, TILES, NBLK, CH = 4, 4, 8, 4
CW = 32
PART = TILES * CW
COPY, IDENT = ActivationFunctionType.Copy, ActivationFunctionType.Identity
UNIT = 2
PIECES = {0: (4, 4), 1: (4, 4), 2: (4, 4), 3: (2, 2, 2, 2)}
XLATE = 3

SCRATCH = {
    "wn": ("sbuf", [128, 2048], "bfloat16"),
    "xb": ("sbuf", [128, 4096], "bfloat16"),
    "xq": ("sbuf", [128, 1024], "float8_e4m3fn_x4"),
    "xs": ("sbuf", [128, 1024], "uint8"),
    "idr": ("sbuf", [128, 32], "int32"),
    "idb": ("sbuf", [128, 32], "int32"),
    "idf": ("sbuf", [128, 32], "float32"),
    "ka": ("sbuf", [128, 32], "int32"),
    "kb": ("sbuf", [128, 32], "int32"),
    "km": ("sbuf", [128, 32], "float32"),
    "pa": ("sbuf", [128, 8], "int32"),
    "pb": ("sbuf", [128, 8], "int32"),
    "ia": ("sbuf", [128, 8], "int32"),
    "pu": ("sbuf", [128, 8], "float32"),
    "ea": ("sbuf", [128, 32], "float32"),
    "eb": ("sbuf", [128, 28], "float32"),
    "sel": ("sbuf", [128, 8], "float32"),
    "offf": ("sbuf", [128, 64], "float32"),
    "off": ("sbuf", [128, 64], "uint16"),
    "ps": ("psum", [128, 4096], "float32"),
}
for _c in range(CH):
    SCRATCH["cw%d" % _c] = ("sbuf", [128, NR * PART], "float8_e4m3fn_x4")
    SCRATCH["cs%d" % _c] = ("sbuf", [128, NR * PART], "uint8")
    SCRATCH["w%d" % _c] = ("sbuf", [128, 512], "bfloat16")
    SCRATCH["pk%d" % _c] = ("sbuf", [128, 1024], "float8_e4m3fn_x4")
    SCRATCH["pp%d" % _c] = ("sbuf", [128, 1024], "uint8")
    SCRATCH["yo%d" % _c] = ("sbuf", [128, 1024], "float32")

SEMAPHORES = ["idl", "wl0", "wl1", "xl0", "xl1", "ga", "va", "sa", "ta", "loc", "out"] \
    + ["hc%d" % c for c in range(CH)] + ["hs%d" % c for c in range(CH)] \
    + ["ac%d" % c for c in range(CH)] + ["as%d" % c for c in range(CH)]


def bits(es):
    return sum(1 << e for e in es)


def part(T, kind, c, r):
    v = T["%s%d" % (kind, c)][:, PART * r:PART * r + PART]
    return v.bitcast(dt.uint8) if kind == "cw" else v


def send(T, topo, kind, c, r, dsts, es, sem):
    ids = []
    for q in dsts:
        rid, pid, _s = topo.addr(q)
        ids.append(DstId(rid=rid, pnc=pid))
    return RemoteDMATransfer(dst_ids=ids, dma_engine_mask=bits(es), remote_sem=T.sem["%s%d" % (sem, c)],
                             srcs=[part(T, kind, c, r)], dsts=[part(T, kind, c, r) for q in dsts])


def others(T, r):
    return [T.cores[(r + i) % NR] for i in range(1, NR)]


def relays(T, topo, r):
    me = T.cores[r]
    ok = [c for c in topo.cores_of(me) if c != me and all(topo.may_write(c, d) for d in others(T, r))]
    near = [c for c in ok if topo.die(c) == topo.die(me)]
    far = [c for c in ok if topo.die(c) != topo.die(me)]
    return far[:2] + near[:1]


def on_chip(T, topo, r):
    me = T.cores[r]
    off = topo.engines(me, others(T, r)[0])
    sp = [e for e in topo.engines(me, relays(T, topo, r)[0]) if e not in off]
    h, q = len(sp) // 2, 3 * len(sp) // 4
    return [[("cw", 2, 0, sp[:h]), ("cw", 3, 1, sp[h:])],
            [("cs", 1, 2, sp[:h]), ("cs", 2, 2, sp[h:q]), ("cs", 3, 1, sp[q:])]]


def relay_program(g, core, T, topo, r, i):
    dsts = others(T, r)
    es = topo.engines(core, dsts[0])
    n = 0
    for call in on_chip(T, topo, r):
        for kind, c, j, got in call:
            if j == i:
                g.wait_ge(T.sem["h%s%d" % (kind[1].replace("w", "c"), c)], len(got))
                g.remote_dma_fused([send(T, topo, kind, c, r, dsts, es, "ac" if kind == "cw" else "as")], local_sem=T.sem.loc)
                n += len(es)
    g.wait_ge(T.sem.loc, n)


def rank_program(g, core, T, topo):
    r = T.rank_of(core)
    if r is None:
        for q in range(NR):
            hs = relays(T, topo, q)
            if core in hs:
                relay_program(g, core, T, topo, q, hs.index(core))
        return
    S = T.sem
    V, A, P, Y = g.vector, g.scalar, g.tensor, g.sync
    nv, na = [0], [0]

    def v(ins):
        ins.then_inc(S.va, 1)
        nv[0] += 1
        return nv[0]

    def a(ins):
        ins.then_inc(S.sa, 1)
        na[0] += 1
        return na[0]

    for m in range(TILES):
        (Y if m < 2 else A).dma_start(T.w0[:, 128 * m:128 * m + 128], T.wt[:, 512 * m:512 * m + 128]).then_inc(S.wl0, 16)
    for m in range(TILES):
        (Y if m < 2 else A).dma_start(T.wn[:, 512 * m + 128:512 * m + 512], T.wt[:, 512 * m + 128:512 * m + 512]).then_inc(S.wl1, 16)
    Y.dma_start(T.idr[0:1, 0:32], T.ids[:, :]).then_inc(S.idl, 16)
    A.dma_start(T.xb[:, 2048:4096], T.x[:, 2048:4096]).then_inc(S.xl1, 16)
    Y.dma_start(T.xb[:, 0:2048], T.x[:, 0:2048]).then_inc(S.xl0, 16)

    dsts = others(T, r)
    hs = relays(T, topo, r)
    far = topo.engines(core, dsts[0])
    g.iota(T.ka[:, :], [[0, 4], [1, 4], [0, 2]], 0, 3).then_inc(S.ga, 1)
    g.iota(T.pa[:, :], [[0, 8]], 0, 1).then_inc(S.ga, 1)
    g.iota(T.ia[:, :], [[4, 8]], 0, 0).then_inc(S.ga, 1)

    V.wait_ge(S.ga, 3)
    v(V.tensor_scalar(T.kb[:, :], T.ka[:, :], 3, None, AluOpType.bitwise_and))
    n = v(V.tensor_scalar(T.pb[:, :], T.pa[:, :], 2, 3, AluOpType.logical_shift_right, AluOpType.bitwise_and))
    V.wait_ge(S.va, n)
    v(V.tensor_scalar(T.km[:, :], T.kb[:, :], 0, CW, AluOpType.is_equal, AluOpType.mult))
    v(V.tensor_tensor(T.pu[:, :], T.pb[:, :], T.ia[:, :], AluOpType.add))

    quant = {}
    cols = slice(PART * r, PART * r + PART)

    def quantise(c):
        quant[c] = v(V.quantize_mx(T["cw%d" % c][:, cols], T["cs%d" % c][:, cols], T["w%d" % c][:, :]))

    V.wait_ge(S.wl0, 16 * TILES)
    quantise(0)
    A.wait_ge(S.wl1, 16 * TILES)
    for m in range(TILES):
        moved = a(A.activation(T.w3[:, 128 * m:128 * m + 128], T.wn[:, 512 * m + 384:512 * m + 512], COPY))
    V.wait_ge(S.wl1, 16 * TILES)
    for c in (2, 3, 1):
        if c != 3:
            for m in range(TILES):
                n = v(V.tensor_copy(T["w%d" % c][:, 128 * m:128 * m + 128], T.wn[:, 512 * m + 128 * c:512 * m + 128 * c + 128]))
            V.wait_ge(S.va, n)
        else:
            V.wait_ge(S.sa, moved)
        quantise(c)

    g.wait_ge(S.va, quant[0])
    g.remote_dma_fused([send(T, topo, "cw", 0, r, dsts, far, "ac")], local_sem=S.loc)
    g.remote_dma_fused([send(T, topo, "cs", 0, r, dsts, far, "as")], local_sem=S.loc)
    left = 3 * len(far)
    for call, c in zip(on_chip(T, topo, r), (3, 1)):
        g.wait_ge(S.va, quant[c])
        g.remote_dma_fused([send(T, topo, kind, k, r, [hs[j]], es, "hc" if kind == "cw" else "hs") for kind, k, j, es in call], local_sem=S.loc)
        left += sum(len(es) for _k, _c, _j, es in call)
    g.remote_dma_fused([send(T, topo, "cw", 1, r, dsts, far, "ac")], local_sem=S.loc)
    g.wait_ge(S.idl, 16)
    g.partition_broadcast(T.idb[:, :], T.idr[0:1, :], 128).then_inc(S.ga, 1)
    g.wait_ge(S.loc, left)

    V.wait_ge(S.ga, 4)
    n = v(V.tensor_copy(T.idf[:, :], T.idb[:, :]))
    V.wait_ge(S.va, n)
    n = v(V.tensor_tensor(T.ea[:, :], T.idf[:, :], T.km[:, :], AluOpType.mult))
    V.wait_ge(S.va, n)
    n = v(V.tensor_tensor(T.eb[:, :], T.ea[:, 0:28], T.ea[:, 4:32], AluOpType.add))
    V.wait_ge(S.va, n)
    for q in range(2):
        n = v(V.tensor_tensor(T.sel[:, 4 * q:4 * q + 4], T.eb[:, q:q + 25:8], T.eb[:, q + 2:q + 27:8], AluOpType.add))
    A.wait_ge(S.va, n)
    for ii in range(8):
        m = a(A.activation(T.offf[:, ii:64:8], T.sel[:, :], IDENT, bias=T.pu[:, ii:ii + 1]))
    xdone = {}

    def quantise_x(q):
        V.wait_ge(S["xl%d" % q], 16)
        cs = slice(512 * q, 512 * q + 512)
        xdone[q] = v(V.quantize_mx(T.xq[:, cs], T.xs[:, cs], T.xb[:, 2048 * q:2048 * q + 2048]))

    quantise_x(0)
    V.wait_ge(S.sa, m)
    listed = v(V.tensor_copy(T.off[:, :], T.offf[:, :]))

    nin = (NR - 1) * len(far)
    pickv, picka, copyv, copya = {}, {}, {}, {}

    def copies(c, b0):
        for b in range(b0, b0 + UNIT):
            o, i = T["yo%d" % c][:, 128 * b:128 * b + 128], T.ps[:, 512 * b:512 * b + 128]
            if b % 2 == 0:
                V.wait_ge(S.ta, NBLK * c + b + 1)
                copyv[c, b] = v(V.tensor_copy(o, i))
            else:
                A.wait_ge(S.ta, NBLK * c + b + 1)
                copya[c, b] = a(A.activation(o, i, COPY))

    V.wait_ge(S.va, listed)
    A.wait_ge(S.va, listed)
    due, picks = [], 0
    for c in range(CH):
        V.wait_ge(S["ac%d" % c], nin)
        A.wait_ge(S["as%d" % c], nin)
        for b0 in range(0, NBLK, UNIT):
            o, to = T.off[:, 8 * b0:8 * b0 + 8 * UNIT], slice(128 * b0, 128 * b0 + 128 * UNIT)
            pickv[c, b0] = v(V.tensor_copy(T["pk%d" % c][:, to].bitcast(dt.uint32), T["cw%d" % c][:, 0:NR * PART].bitcast(dt.uint32).indirect(o)))
            picka[c, b0] = a(A.activation(T["pp%d" % c][:, to], T["cs%d" % c][:, 0:NR * PART].indirect(o), COPY))
            picks += 1
            if picks == XLATE:
                quantise_x(1)
            for d in due:
                copies(*d)
            due = [(c, b0)]
    for d in due:
        copies(*d)

    for c in range(CH):
        for b0 in range(0, NBLK, UNIT):
            P.wait_ge(S.va, max(pickv[c, b0], xdone[2 * b0 // NBLK]))
            P.wait_ge(S.sa, picka[c, b0])
            for b in range(b0, b0 + UNIT):
                if c:
                    if b % 2 == 0:
                        P.wait_ge(S.va, copyv[c - 1, b])
                    else:
                        P.wait_ge(S.sa, copya[c - 1, b])
                cs = slice(128 * b, 128 * b + 128)
                P.matmul_mx(T.ps[:, 512 * b:512 * b + 128], T["pk%d" % c][:, cs], T["pp%d" % c][:, cs],
                            T.xq[:, cs], T.xs[:, cs], True, True).then_inc(S.ta, 1)

    nout = 0
    for c in range(CH):
        b0 = 0
        for nb in PIECES[c]:
            last = c == CH - 1 and b0 + nb == NBLK
            for q in (Y, A) if last else (Y,):
                q.wait_ge(S.va, copyv[c, b0 + nb - 2])
                q.wait_ge(S.sa, copya[c, b0 + nb - 1])
            for k in range(4):
                (A if last and k % 2 else Y).dma_start(
                    T.y[32 * c:32 * c + 32, 1024 * k + 128 * b0:1024 * k + 128 * (b0 + nb)],
                    T["yo%d" % c][k:128:4, 128 * b0:128 * (b0 + nb)]).then_inc(S.out, 16)
                nout += 1
            b0 += nb
    Y.wait_ge(S.ta, NBLK * CH)
    Y.wait_ge(S.out, 16 * nout)
